import numpy as np
import ml_dtypes


def mxq(x, axis, fmt="e4m3"):
    dtype, down = {"e4m3": (ml_dtypes.float8_e4m3fn, 7), "e5m2": (ml_dtypes.float8_e5m2, 14)}[fmt]
    v = np.moveaxis(np.asarray(x, np.float32).astype(ml_dtypes.bfloat16).astype(np.float64), axis, -1)
    blocks = v.reshape(v.shape[:-1] + (-1, 32))
    amax = np.abs(blocks).max(-1, keepdims=True)
    byte = np.maximum(np.where(amax > 0, np.frexp(amax)[1] - 1 + 127, 0) - down, 1)
    scale = np.exp2(byte - 127.0)
    codes = (blocks / scale).astype(np.float32).astype(dtype).astype(np.float64)
    return np.moveaxis((codes * scale).reshape(v.shape), -1, axis)


WIDE = False


def mx_kscale(k):
    if not WIDE:
        return np.ones(k)
    levels = np.array([30, -30])
    if k % 512:
        return np.exp2(np.random.permutation(np.resize(levels, k // 32))).repeat(32)
    a = np.empty((k // 512, 16))
    for p in range(k // 512):
        a[p, :8] = np.random.permutation(np.resize(levels, 8))
        for g in range(8):
            far = levels[np.abs(levels - a[p, g]) >= 10]
            a[p, g + 8] = far[np.random.randint(len(far))]
    return np.exp2(a.ravel()).repeat(32)


def f64(x):
    return np.asarray(x).astype(np.float64)


def striped(idx):
    return np.tile(np.asarray(idx).reshape(-1, 16).T, (8, 1)).astype(np.uint16)


def unstriped(offs):
    return offs[:16].T.reshape(-1).astype(np.int64)


def striped8(idx):
    return np.asarray(idx).reshape(8, -1, 16).transpose(0, 2, 1).reshape(128, -1).astype(np.uint16)


def unstriped8(offs):
    return offs.reshape(8, 16, -1).transpose(0, 2, 1).reshape(8, -1).astype(np.int64)


def pick8(x, idx, run):
    r = np.arange(len(x))
    return x[r[:, None], idx[r % (8 * run) // run]]


E2M1 = np.array([0.0, 0.5, 1.0, 1.5, 2.0, 3.0, 4.0, 6.0, -0.0, -0.5, -1.0, -1.5, -2.0, -3.0, -4.0, -6.0])


def pack_weight(w, fmt):
    k, n = w.shape
    w = f64(np.asarray(w, np.float32).astype(ml_dtypes.bfloat16)).reshape(k // 32, 32, n)
    amax = np.abs(w).max(1)
    if fmt in ("e4m3", "e5m2"):
        byte = np.frexp(amax)[1] - 1 + 127 - (7 if fmt == "e4m3" else 14)
    else:
        mant, ex = np.frexp(amax / 6.0)
        byte = np.where(mant > 0.5, ex, ex - 1) + 127
    byte = np.clip(np.where(amax > 0, byte, 1), 1, 254)
    scaled = (w * np.exp2(127.0 - byte)[:, None, :]).reshape(k, n).astype(np.float32)
    by_word = np.ascontiguousarray(scaled.reshape(k // 512, 128, 4, n).transpose(0, 1, 3, 2))
    if fmt in ("e4m3", "e5m2"):
        words = by_word.astype(ml_dtypes.float8_e4m3fn if fmt == "e4m3" else ml_dtypes.float8_e5m2).view(np.uint8)
    else:
        c = by_word.astype(ml_dtypes.float4_e2m1fn).view(np.uint8) & 0xF
        words = (c[..., 0::2] | (c[..., 1::2] << 4)).reshape(k // 512, 128, 2 * n)
    return np.ascontiguousarray(words), np.ascontiguousarray(byte.astype(np.uint8).reshape(k // 512, 16, n))


def unpack_weight(words, scales, fmt):
    g, _, n = scales.shape
    words = np.ascontiguousarray(words).reshape(g, 128, n, -1)
    if fmt in ("e4m3", "e5m2"):
        vals = words.view(ml_dtypes.float8_e4m3fn if fmt == "e4m3" else ml_dtypes.float8_e5m2).astype(np.float64)
    else:
        nib = np.empty((g, 128, n, 4), np.uint8)
        nib[..., 0::2] = words & 0xF
        nib[..., 1::2] = words >> 4
        vals = E2M1[nib]
    vals = vals * np.repeat(np.exp2(scales.astype(np.float64) - 127.0), 8, axis=1)[..., None]
    return vals.transpose(0, 1, 3, 2).reshape(g * 512, n)


def sigmoid(v):
    return 1.0 / (1.0 + np.exp(-v))


def sgn(shape):
    return np.random.uniform(0.5, 2.0, shape) * np.where(np.random.standard_normal(shape) < 0, -1.0, 1.0)


K, T, J, R, V, C, O, N, E = 512, 1024, 256, 512, 1024, 512, 256, 256, 512


def setup_inputs():
    n = np.random.standard_normal
    idx = np.random.permutation(V)[:R]
    idx2 = np.random.permutation(T)[:J]
    idx3 = np.stack([np.random.permutation(C)[:J] for _ in range(8)])
    idx4 = np.stack([np.random.permutation(C)[:O] for _ in range(8)])
    idx5 = np.stack([np.random.permutation(C)[:O] for _ in range(8)])
    idx6 = np.random.permutation(E)[:O]
    idx7 = np.random.permutation(E)[:O]
    fk = mx_kscale(K)
    fr = mx_kscale(R)
    xtp = pack_weight(n((K, T)) / fk[:, None], "e5m2")
    wtp = pack_weight(n((K, V)) * 1 / np.sqrt(K) * fk[:, None], "e2m1")
    wbp = pack_weight(n((R, N)) * 1 / np.sqrt(R) / fr[:, None], "e2m1")
    return {
        "xt_words": xtp[0],
        "xt_scales": xtp[1],
        "wt_words": wtp[0],
        "wt_scales": wtp[1],
        "sa": (np.random.uniform(0.5, 1.6, (R, 1)) * fr[:, None]).astype(np.float32),
        "sg": (sgn((R, 1))).astype(np.float32),
        "bg": (np.random.uniform(-2.0, 2.0, (R, 1))).astype(np.float32),
        "wb_words": wbp[0],
        "wb_scales": wbp[1],
        "offs": striped(idx),
        "offs2": striped(idx2),
        "offs3": striped8(idx3),
        "offs4": striped8(idx4),
        "offs5": striped8(idx5),
        "offs6": striped(idx6),
        "offs7": striped(idx7),
    }


def reference(xt_words, xt_scales, wt_words, wt_scales, sa, sg, bg, wb_words, wb_scales, offs, offs2, offs3, offs4, offs5, offs6, offs7):
    idx = unstriped(offs)
    idx2 = unstriped(offs2)
    idx3 = unstriped8(offs3)
    idx4 = unstriped8(offs4)
    idx5 = unstriped8(offs5)
    idx6 = unstriped(offs6)
    idx7 = unstriped(offs7)
    xtu = unpack_weight(xt_words, xt_scales, "e5m2")
    wtu = unpack_weight(wt_words, wt_scales, "e2m1")
    wbu = unpack_weight(wb_words, wb_scales, "e2m1")
    wtidxg = wtu[:, idx]
    xtidx2g = xtu[:, idx2]
    a = wtidxg.T @ xtidx2g
    pw = np.zeros((R, C))
    pw[np.arange(R)[:, None], idx3[np.arange(R) % 512 // 64]] = a
    hid = pick8(pw, idx4, 64) * f64(sa) * sigmoid(pick8(pw, idx5, 64) * f64(sg) + f64(bg))
    hidq = mxq(hid, 0, "e4m3")
    p = wbu.T @ hidq
    pa = np.zeros((N, E))
    pa[:, idx6] = p
    pb = np.zeros((N, E))
    pb[:, idx7] = p
    y = pa + pb
    return y

@@ -1,0 +1,190 @@
+from contextlib import ExitStack
+
+import concourse.mybir as mybir
+
+K, T, J, R, V, C, O, N, E = 512, 1024, 256, 512, 1024, 512, 256, 256, 512
+FLOPS = 2 * K * R * J + 2 * R * N * O
+
+F32 = mybir.dt.float32
+BF16 = mybir.dt.bfloat16
+I32 = mybir.dt.int32
+U32 = mybir.dt.uint32
+U16 = mybir.dt.uint16
+U8 = mybir.dt.uint8
+E4M3 = mybir.dt.float8_e4m3fn_x4
+E5M2 = mybir.dt.float8_e5m2_x4
+E2M1 = mybir.dt.float4_e2m1fn_x4
+ACT = mybir.ActivationFunctionType
+ALU = mybir.AluOpType
+
+P = 128
+PACK = 4
+QUAD = 32
+HALF = O // 2
+LIST_ROWS = 16
+MID = 4 * (PACK - 1) * O
+
+
+def tile_list_gatedgroupboard_chosen_one_pagetwice_kernel(
+    tc, xt_words, xt_scales, wt_words, wt_scales, sa, sg, bg, wb_words, wb_scales,
+    offs, offs2, offs3, offs4, offs5, offs6, offs7, out,
+):
+    nc = tc.nc
+    with ExitStack() as ctx:
+        keep = ctx.enter_context(tc.tile_pool(name="keep", bufs=1))
+        turns = ctx.enter_context(tc.tile_pool(name="turns", bufs=1))
+        psum = ctx.enter_context(tc.psum_pool(name="psum", bufs=1))
+
+        def load_list(name, src):
+            tile = keep.tile(list(src.shape), U16, name=name)
+            nc.sync.dma_start(tile[:], src)
+            return tile
+
+        def load_scale_window(tile, src):
+            rows = src[0].bitcast(I32)
+            for q in range(P // QUAD):
+                nc.sync.dma_start(
+                    tile[QUAD * q : QUAD * (q + 1), :].bitcast(I32),
+                    rows[PACK * q : PACK * (q + 1), :].partition_broadcast(QUAD // PACK),
+                )
+
+        def load_by_row(name, src):
+            tile = keep.tile([P, PACK], F32, name=name)
+            nc.sync.dma_start(tile[:], src.rearrange("(p t) one -> p (t one)", t=PACK))
+            return tile
+
+        wt_w = keep.tile([P, V], U16, name="wt_w")
+        nc.sync.dma_start(wt_w[:].bitcast(I32), wt_words[0].bitcast(I32))
+        list1 = load_list("list1", offs)
+        wt_sc = keep.tile([P, V], U8, name="wt_sc")
+        load_scale_window(wt_sc, wt_scales)
+        list2 = load_list("list2", offs2)
+        xt_w = keep.tile([P, T], I32, name="xt_w")
+        nc.sync.dma_start(xt_w[:], xt_words[0].rearrange("p n t -> p (n t)").bitcast(I32))
+        xt_sc = turns.tile([P, T], U8, name="xt_sc", offset=MID - T // 2)
+        load_scale_window(xt_sc, xt_scales)
+        list3 = load_list("list3", offs3)
+        list4 = load_list("list4", offs4)
+        list5 = load_list("list5", offs5)
+        sa_t = load_by_row("sa_t", sa)
+        sg_t = load_by_row("sg_t", sg)
+        bg_t = load_by_row("bg_t", bg)
+
+        boards = [keep.tile([P, C], F32, name="board%d" % t) for t in range(PACK)]
+        pages_a = [keep.tile([P, E], F32, name="page_a%d" % b) for b in range(N // P)]
+        pages_b = [keep.tile([P, E], F32, name="page_b%d" % b) for b in range(N // P)]
+        wb_sc = keep.tile([P, N], U8, name="wb_sc", align_bytes=64)
+        nc.vector.memset(wb_sc[:].bitcast(I32), 0)
+        for tile in boards + pages_a + pages_b:
+            nc.vector.memset(tile[:].bitcast(I32), 0)
+
+        wb_w = keep.tile([P, N], U16, name="wb_w", align_bytes=64)
+        nc.sync.dma_start(wb_w[:].bitcast(I32), wb_words[0].bitcast(I32))
+        wb_rows = wb_scales[0].bitcast(I32)
+        for q in range(P // QUAD):
+            nc.sync.dma_start(
+                wb_sc[QUAD * q : QUAD * q + PACK, :].bitcast(I32), wb_rows[PACK * q : PACK * (q + 1), :]
+            )
+        list6 = load_list("list6", offs6)
+        list7 = load_list("list7", offs7)
+
+        wt_w_g = keep.tile([P, R], U16, name="wt_w_g")
+        nc.vector.tensor_copy(wt_w_g[:], wt_w[:].indirect(list1[:]))
+        wt_sc_g = keep.tile([P, R], U8, name="wt_sc_g")
+        nc.vector.tensor_copy(wt_sc_g[:], wt_sc[:].indirect(list1[:]))
+        xt_w_g = keep.tile([P, J], U32, name="xt_w_g", align_bytes=64)
+        nc.vector.tensor_copy(xt_w_g[:], xt_w[:].bitcast(U32).indirect(list2[:]))
+        xt_sc_g = keep.tile([P, J], U8, name="xt_sc_g", align_bytes=64)
+        nc.vector.tensor_copy(xt_sc_g[:], xt_sc[:].indirect(list2[:]))
+
+        wt_w_first = keep.tile([P, 1, P], U16, name="wt_w_first", align_bytes=64)
+        wt_sc_first = keep.tile([P, 1, P], U8, name="wt_sc_first", align_bytes=64)
+        wt_w_rest = turns.tile([P, PACK - 1, P], U16, name="wt_w_rest", offset=MID - 2 * (PACK - 1) * P, align_bytes=64)
+        wt_sc_rest = turns.tile([P, PACK - 1, P], U8, name="wt_sc_rest", offset=MID, align_bytes=64)
+        w_by_t = wt_w_g[:].rearrange("p (m t) -> p t m", t=PACK)
+        sc_by_t = wt_sc_g[:].rearrange("p (m t) -> p t m", t=PACK)
+        nc.vector.tensor_copy(wt_w_first[:], w_by_t[:, 0:1, :])
+        nc.vector.tensor_copy(wt_sc_first[:], sc_by_t[:, 0:1, :])
+        nc.vector.tensor_copy(wt_w_rest[:], w_by_t[:, 1:PACK, :])
+        nc.vector.tensor_copy(wt_sc_rest[:], sc_by_t[:, 1:PACK, :])
+
+        gate = turns.tile([P, PACK - 1, O], F32, name="gate", offset=0)
+        picked = turns.tile([P, PACK - 1, O], F32, name="picked", offset=MID)
+        gate_last = [keep.tile([P, HALF], F32, name="gate_last%d" % h) for h in range(2)]
+        picked_last = [keep.tile([P, HALF], F32, name="picked_last%d" % h) for h in range(2)]
+
+        def look(t, lo, hi, gate_out, picked_out):
+            cols = slice(lo // LIST_ROWS, hi // LIST_ROWS)
+            nc.scalar.activation(
+                out=gate_out, in_=boards[t][:].indirect(list5[:, cols]), func=ACT.Sigmoid,
+                bias=bg_t[:, t : t + 1], scale=sg_t[:, t : t + 1],
+            )
+            nc.scalar.activation(
+                out=picked_out, in_=boards[t][:].indirect(list4[:, cols]), func=ACT.Copy,
+                scale=sa_t[:, t : t + 1],
+            )
+
+        a_sb = []
+        for t in range(PACK):
+            words = wt_w_first[:, 0, :] if t == 0 else wt_w_rest[:, t - 1, :]
+            scales = wt_sc_first[:, 0, :] if t == 0 else wt_sc_rest[:, t - 1, :]
+            acc = psum.tile([P, J], F32, name="acc_a%d" % t)
+            nc.tensor.matmul_mx(
+                out=acc[:], lhsT=words.bitcast(E2M1), lhsT_scale=scales,
+                rhs=xt_w_g[:].bitcast(E5M2), rhs_scale=xt_sc_g[:], start=True, stop=True,
+            )
+            rows = keep.tile([P, J], F32, name="a_sb%d" % t)
+            nc.scalar.copy(rows[:], acc[:])
+            a_sb.append(rows)
+        for t in range(PACK):
+            nc.vector.tensor_copy(boards[t][:].indirect(list3[:]), a_sb[t][:])
+            if t < PACK - 1:
+                look(t, 0, O, gate[:, t, :], picked[:, t, :])
+        for h in range(2):
+            look(PACK - 1, h * HALF, (h + 1) * HALF, gate_last[h][:], picked_last[h][:])
+
+        hid = [keep.tile([P, HALF * PACK], BF16, name="hid%d" % h, align_bytes=64) for h in range(2)]
+        for h in range(2):
+            cols = slice(h * HALF, (h + 1) * HALF)
+            nc.vector.tensor_tensor(
+                hid[h][:].rearrange("p (c i t) -> p c t i", i=4, t=PACK)[:, :, 0 : PACK - 1, :],
+                picked[:, :, cols].rearrange("p t (c i) -> p c t i", i=4),
+                gate[:, :, cols].rearrange("p t (c i) -> p c t i", i=4),
+                ALU.mult,
+            )
+
+        p_sb = [keep.tile([P, N // P, HALF], F32, name="p_sb%d" % h) for h in range(2)]
+        for h in range(2):
+            nc.vector.tensor_tensor(
+                hid[h][:].rearrange("p (o t) -> p o t", t=PACK)[:, :, PACK - 1],
+                picked_last[h][:], gate_last[h][:], ALU.mult,
+            )
+            codes = keep.tile([P, HALF], U32, name="codes%d" % h, align_bytes=64)
+            code_sc = keep.tile([P, HALF], U8, name="code_sc%d" % h, align_bytes=64)
+            nc.vector.quantize_mx(out=codes[:].bitcast(E4M3), scales=code_sc[:], in_=hid[h][:])
+            if h == 0:
+                accs = [psum.tile([P, HALF], F32, name="acc_p0_%d" % b)[:] for b in range(N // P)]
+            else:
+                acc_both = psum.tile([P, N // P, HALF], F32, name="acc_p1")
+                accs = [acc_both[:, b, :] for b in range(N // P)]
+            for b in range(N // P):
+                nc.tensor.matmul_mx(
+                    out=accs[b], lhsT=wb_w[:, b * P : (b + 1) * P].bitcast(E2M1),
+                    lhsT_scale=wb_sc[:, b * P : (b + 1) * P],
+                    rhs=codes[:].bitcast(E4M3), rhs_scale=code_sc[:], start=True, stop=True,
+                )
+                if h == 0:
+                    nc.scalar.copy(p_sb[h][:, b, :], accs[b])
+            if h == 1:
+                nc.scalar.copy(p_sb[h][:], acc_both[:])
+
+        for h in range(2):
+            cols = slice(h * HALF // LIST_ROWS, (h + 1) * HALF // LIST_ROWS)
+            for b in range(N // P):
+                nc.vector.tensor_copy(pages_a[b][:].indirect(list6[:, cols]), p_sb[h][:, b, :])
+                nc.scalar.activation(out=pages_b[b][:].indirect(list7[:, cols]), in_=p_sb[h][:, b, :], func=ACT.Copy)
+
+        for b, lo, hi in ((0, 0, E), (1, 0, E // 2), (1, E // 2, E)):
+            total = keep.tile([P, hi - lo], F32, name="total%d_%d" % (b, lo))
+            nc.vector.tensor_tensor(total[:], pages_a[b][:, lo:hi], pages_b[b][:, lo:hi], ALU.add)
+            nc.sync.dma_start(out[b * P : (b + 1) * P, lo:hi], total[:])

@@ -22,7 +22,6 @@ PACK = 4
 QUAD = 32
 HALF = O // 2
 LIST_ROWS = 16
-MID = 4 * (PACK - 1) * O
 
 
 def tile_list_gatedgroupboard_chosen_one_pagetwice_kernel(
@@ -48,10 +47,10 @@ def tile_list_gatedgroupboard_chosen_one_pagetwice_kernel(
                     rows[PACK * q : PACK * (q + 1), :].partition_broadcast(QUAD // PACK),
                 )
 
-        def load_by_row(name, src):
-            tile = keep.tile([P, PACK], F32, name=name)
-            nc.sync.dma_start(tile[:], src.rearrange("(p t) one -> p (t one)", t=PACK))
-            return tile
+        warm_in = keep.tile([P, 1], F32, name="warm_in")
+        warm_out = keep.tile([P, 1], F32, name="warm_out")
+        nc.gpsimd.memset(warm_in[:], 0.0)
+        nc.scalar.activation(out=warm_out[:], in_=warm_in[:], func=ACT.Sigmoid)
 
         wt_w = keep.tile([P, V], U16, name="wt_w")
         nc.sync.dma_start(wt_w[:].bitcast(I32), wt_words[0].bitcast(I32))
@@ -59,24 +58,24 @@ def tile_list_gatedgroupboard_chosen_one_pagetwice_kernel(
         wt_sc = keep.tile([P, V], U8, name="wt_sc")
         load_scale_window(wt_sc, wt_scales)
         list2 = load_list("list2", offs2)
-        xt_w = keep.tile([P, T], I32, name="xt_w")
+        xt_w = turns.tile([P, T], I32, name="xt_w", offset=8192)
         nc.sync.dma_start(xt_w[:], xt_words[0].rearrange("p n t -> p (n t)").bitcast(I32))
-        xt_sc = turns.tile([P, T], U8, name="xt_sc", offset=MID - T // 2)
+        xt_sc = turns.tile([P, T], U8, name="xt_sc", offset=512)
         load_scale_window(xt_sc, xt_scales)
         list3 = load_list("list3", offs3)
         list4 = load_list("list4", offs4)
         list5 = load_list("list5", offs5)
-        sa_t = load_by_row("sa_t", sa)
-        sg_t = load_by_row("sg_t", sg)
-        bg_t = load_by_row("bg_t", bg)
+
+        loaded = keep.tile([P, 3, 2 * PACK], F32, name="loaded")
+        nc.gpsimd.dma_start(loaded[:, 0, 0:PACK], sa.rearrange("(p t) one -> p (t one)", t=PACK))
 
         boards = [keep.tile([P, C], F32, name="board%d" % t) for t in range(PACK)]
         pages_a = [keep.tile([P, E], F32, name="page_a%d" % b) for b in range(N // P)]
         pages_b = [keep.tile([P, E], F32, name="page_b%d" % b) for b in range(N // P)]
         wb_sc = keep.tile([P, N], U8, name="wb_sc", align_bytes=64)
-        nc.vector.memset(wb_sc[:].bitcast(I32), 0)
+        nc.gpsimd.memset(wb_sc[:].bitcast(I32), 0)
         for tile in boards + pages_a + pages_b:
-            nc.vector.memset(tile[:].bitcast(I32), 0)
+            nc.gpsimd.memset(tile[:], 0.0)
 
         wb_w = keep.tile([P, N], U16, name="wb_w", align_bytes=64)
         nc.sync.dma_start(wb_w[:].bitcast(I32), wb_words[0].bitcast(I32))
@@ -87,6 +86,10 @@ def tile_list_gatedgroupboard_chosen_one_pagetwice_kernel(
             )
         list6 = load_list("list6", offs6)
         list7 = load_list("list7", offs7)
+        for i, src in ((1, sg), (2, bg)):
+            nc.sync.dma_start(loaded[:, i, 0:PACK], src.rearrange("(p t) one -> p (t one)", t=PACK))
+        consts = keep.tile([P, 3, PACK], F32, name="consts")
+        nc.gpsimd.tensor_copy(consts[:], loaded[:, :, 0:PACK])
 
         wt_w_g = keep.tile([P, R], U16, name="wt_w_g")
         nc.vector.tensor_copy(wt_w_g[:], wt_w[:].indirect(list1[:]))
@@ -97,10 +100,10 @@ def tile_list_gatedgroupboard_chosen_one_pagetwice_kernel(
         xt_sc_g = keep.tile([P, J], U8, name="xt_sc_g", align_bytes=64)
         nc.vector.tensor_copy(xt_sc_g[:], xt_sc[:].indirect(list2[:]))
 
-        wt_w_first = keep.tile([P, 1, P], U16, name="wt_w_first", align_bytes=64)
-        wt_sc_first = keep.tile([P, 1, P], U8, name="wt_sc_first", align_bytes=64)
-        wt_w_rest = turns.tile([P, PACK - 1, P], U16, name="wt_w_rest", offset=MID - 2 * (PACK - 1) * P, align_bytes=64)
-        wt_sc_rest = turns.tile([P, PACK - 1, P], U8, name="wt_sc_rest", offset=MID, align_bytes=64)
+        wt_w_first = turns.tile([P, 1, P], U16, name="wt_w_first", offset=8192, align_bytes=64)
+        wt_sc_first = turns.tile([P, 1, P], U8, name="wt_sc_first", offset=8192 + 256, align_bytes=64)
+        wt_w_rest = turns.tile([P, PACK - 1, P], U16, name="wt_w_rest", offset=0, align_bytes=64)
+        wt_sc_rest = turns.tile([P, PACK - 1, P], U8, name="wt_sc_rest", offset=768, align_bytes=64)
         w_by_t = wt_w_g[:].rearrange("p (m t) -> p t m", t=PACK)
         sc_by_t = wt_sc_g[:].rearrange("p (m t) -> p t m", t=PACK)
         nc.vector.tensor_copy(wt_w_first[:], w_by_t[:, 0:1, :])
@@ -108,20 +111,18 @@ def tile_list_gatedgroupboard_chosen_one_pagetwice_kernel(
         nc.vector.tensor_copy(wt_w_rest[:], w_by_t[:, 1:PACK, :])
         nc.vector.tensor_copy(wt_sc_rest[:], sc_by_t[:, 1:PACK, :])
 
-        gate = turns.tile([P, PACK - 1, O], F32, name="gate", offset=0)
-        picked = turns.tile([P, PACK - 1, O], F32, name="picked", offset=MID)
-        gate_last = [keep.tile([P, HALF], F32, name="gate_last%d" % h) for h in range(2)]
-        picked_last = [keep.tile([P, HALF], F32, name="picked_last%d" % h) for h in range(2)]
+        looked = turns.tile([P, 2, PACK, O], F32, name="looked", offset=0)
+        last = keep.tile([P, 2, HALF], F32, name="last", tag="last", align_bytes=64)
 
         def look(t, lo, hi, gate_out, picked_out):
             cols = slice(lo // LIST_ROWS, hi // LIST_ROWS)
             nc.scalar.activation(
                 out=gate_out, in_=boards[t][:].indirect(list5[:, cols]), func=ACT.Sigmoid,
-                bias=bg_t[:, t : t + 1], scale=sg_t[:, t : t + 1],
+                bias=consts[:, 2, t : t + 1], scale=consts[:, 1, t : t + 1],
             )
             nc.scalar.activation(
                 out=picked_out, in_=boards[t][:].indirect(list4[:, cols]), func=ACT.Copy,
-                scale=sa_t[:, t : t + 1],
+                scale=consts[:, 0, t : t + 1],
             )
 
         a_sb = []
@@ -139,50 +140,52 @@ def tile_list_gatedgroupboard_chosen_one_pagetwice_kernel(
         for t in range(PACK):
             nc.vector.tensor_copy(boards[t][:].indirect(list3[:]), a_sb[t][:])
             if t < PACK - 1:
-                look(t, 0, O, gate[:, t, :], picked[:, t, :])
-        for h in range(2):
-            look(PACK - 1, h * HALF, (h + 1) * HALF, gate_last[h][:], picked_last[h][:])
+                look(t, 0, O, looked[:, 0, t, :], looked[:, 1, t, :])
+        look(PACK - 1, 0, HALF, last[:, 0, :], last[:, 1, :])
+        look(PACK - 1, HALF, O, looked[:, 0, PACK - 1, HALF:O], looked[:, 1, PACK - 1, HALF:O])
 
-        hid = [keep.tile([P, HALF * PACK], BF16, name="hid%d" % h, align_bytes=64) for h in range(2)]
-        for h in range(2):
-            cols = slice(h * HALF, (h + 1) * HALF)
+        def product(hid, cols, slots):
             nc.vector.tensor_tensor(
-                hid[h][:].rearrange("p (c i t) -> p c t i", i=4, t=PACK)[:, :, 0 : PACK - 1, :],
-                picked[:, :, cols].rearrange("p t (c i) -> p c t i", i=4),
-                gate[:, :, cols].rearrange("p t (c i) -> p c t i", i=4),
+                hid[:].rearrange("p (c i t) -> p c t i", i=4, t=PACK)[:, :, 0:slots, :],
+                looked[:, 1, 0:slots, cols].rearrange("p t (c i) -> p c t i", i=4),
+                looked[:, 0, 0:slots, cols].rearrange("p t (c i) -> p c t i", i=4),
                 ALU.mult,
             )
 
-        p_sb = [keep.tile([P, N // P, HALF], F32, name="p_sb%d" % h) for h in range(2)]
+        p_sb = [turns.tile([P, O], F32, name="p_sb0", offset=0), keep.tile([P, O], F32, name="p_sb1")]
+        acc_p1 = psum.tile([P, O], F32, name="acc_p1")
+
+        def put(b, lo, hi):
+            cols = slice(lo // LIST_ROWS, hi // LIST_ROWS)
+            nc.vector.tensor_copy(pages_a[b][:].indirect(list6[:, cols]), p_sb[b][:, lo:hi])
+            nc.scalar.activation(out=pages_b[b][:].indirect(list7[:, cols]), in_=p_sb[b][:, lo:hi], func=ACT.Copy)
+
         for h in range(2):
-            nc.vector.tensor_tensor(
-                hid[h][:].rearrange("p (o t) -> p o t", t=PACK)[:, :, PACK - 1],
-                picked_last[h][:], gate_last[h][:], ALU.mult,
-            )
+            if h == 0:
+                hid = keep.tile([P, HALF * PACK], BF16, name="hid0", align_bytes=64)
+                product(hid, slice(0, HALF), PACK - 1)
+                nc.vector.tensor_tensor(
+                    hid[:].rearrange("p (o t) -> p o t", t=PACK)[:, :, PACK - 1], last[:, 1, :], last[:, 0, :], ALU.mult
+                )
+            else:
+                hid = keep.tile([P, HALF * PACK], BF16, name="hid1", tag="last", align_bytes=64)
+                product(hid, slice(HALF, O), PACK)
             codes = keep.tile([P, HALF], U32, name="codes%d" % h, align_bytes=64)
             code_sc = keep.tile([P, HALF], U8, name="code_sc%d" % h, align_bytes=64)
-            nc.vector.quantize_mx(out=codes[:].bitcast(E4M3), scales=code_sc[:], in_=hid[h][:])
-            if h == 0:
-                accs = [psum.tile([P, HALF], F32, name="acc_p0_%d" % b)[:] for b in range(N // P)]
-            else:
-                acc_both = psum.tile([P, N // P, HALF], F32, name="acc_p1")
-                accs = [acc_both[:, b, :] for b in range(N // P)]
-            for b in range(N // P):
+            nc.vector.quantize_mx(out=codes[:].bitcast(E4M3), scales=code_sc[:], in_=hid[:])
+            cols = slice(h * HALF, (h + 1) * HALF)
+            acc_p0 = psum.tile([P, HALF], F32, name="acc_p0_%d" % h)
+            for b, bank in enumerate((acc_p0[:], acc_p1[:, cols])):
                 nc.tensor.matmul_mx(
-                    out=accs[b], lhsT=wb_w[:, b * P : (b + 1) * P].bitcast(E2M1),
+                    out=bank, lhsT=wb_w[:, b * P : (b + 1) * P].bitcast(E2M1),
                     lhsT_scale=wb_sc[:, b * P : (b + 1) * P],
                     rhs=codes[:].bitcast(E4M3), rhs_scale=code_sc[:], start=True, stop=True,
                 )
-                if h == 0:
-                    nc.scalar.copy(p_sb[h][:, b, :], accs[b])
+            nc.scalar.copy(p_sb[0][:, cols], acc_p0[:])
             if h == 1:
-                nc.scalar.copy(p_sb[h][:], acc_both[:])
-
-        for h in range(2):
-            cols = slice(h * HALF // LIST_ROWS, (h + 1) * HALF // LIST_ROWS)
-            for b in range(N // P):
-                nc.vector.tensor_copy(pages_a[b][:].indirect(list6[:, cols]), p_sb[h][:, b, :])
-                nc.scalar.activation(out=pages_b[b][:].indirect(list7[:, cols]), in_=p_sb[h][:, b, :], func=ACT.Copy)
+                nc.scalar.copy(p_sb[1][:], acc_p1[:])
+            put(0, h * HALF, (h + 1) * HALF)
+        put(1, 0, O)
 
         for b, lo, hi in ((0, 0, E), (1, 0, E // 2), (1, E // 2, E)):
             total = keep.tile([P, hi - lo], F32, name="total%d_%d" % (b, lo))

@@ -73,9 +73,9 @@ def tile_list_gatedgroupboard_chosen_one_pagetwice_kernel(
         pages_a = [keep.tile([P, E], F32, name="page_a%d" % b) for b in range(N // P)]
         pages_b = [keep.tile([P, E], F32, name="page_b%d" % b) for b in range(N // P)]
         wb_sc = keep.tile([P, N], U8, name="wb_sc", align_bytes=64)
-        nc.gpsimd.memset(wb_sc[:].bitcast(I32), 0)
+        nc.vector.memset(wb_sc[:].bitcast(I32), 0)
         for tile in boards + pages_a + pages_b:
-            nc.gpsimd.memset(tile[:], 0.0)
+            nc.vector.memset(tile[:].bitcast(I32), 0)
 
         wb_w = keep.tile([P, N], U16, name="wb_w", align_bytes=64)
         nc.sync.dma_start(wb_w[:].bitcast(I32), wb_words[0].bitcast(I32))
@@ -152,14 +152,18 @@ def tile_list_gatedgroupboard_chosen_one_pagetwice_kernel(
                 ALU.mult,
             )
 
-        p_sb = [turns.tile([P, O], F32, name="p_sb0", offset=0), keep.tile([P, O], F32, name="p_sb1")]
-        acc_p1 = psum.tile([P, O], F32, name="acc_p1")
+        p_sb = turns.tile([P, N // P, O], F32, name="p_sb", offset=0)
 
-        def put(b, lo, hi):
-            cols = slice(lo // LIST_ROWS, hi // LIST_ROWS)
-            nc.vector.tensor_copy(pages_a[b][:].indirect(list6[:, cols]), p_sb[b][:, lo:hi])
-            nc.scalar.activation(out=pages_b[b][:].indirect(list7[:, cols]), in_=p_sb[b][:, lo:hi], func=ACT.Copy)
+        def put_a(b, lo, hi):
+            nc.vector.tensor_copy(pages_a[b][:].indirect(list6[:, lo // LIST_ROWS : hi // LIST_ROWS]), p_sb[:, b, lo:hi])
 
+        def put_b(b, lo, hi):
+            nc.scalar.activation(
+                out=pages_b[b][:].indirect(list7[:, lo // LIST_ROWS : hi // LIST_ROWS]), in_=p_sb[:, b, lo:hi],
+                func=ACT.Copy,
+            )
+
+        accs = []
         for h in range(2):
             if h == 0:
                 hid = keep.tile([P, HALF * PACK], BF16, name="hid0", align_bytes=64)
@@ -173,19 +177,28 @@ def tile_list_gatedgroupboard_chosen_one_pagetwice_kernel(
             codes = keep.tile([P, HALF], U32, name="codes%d" % h, align_bytes=64)
             code_sc = keep.tile([P, HALF], U8, name="code_sc%d" % h, align_bytes=64)
             nc.vector.quantize_mx(out=codes[:].bitcast(E4M3), scales=code_sc[:], in_=hid[:])
-            cols = slice(h * HALF, (h + 1) * HALF)
-            acc_p0 = psum.tile([P, HALF], F32, name="acc_p0_%d" % h)
-            for b, bank in enumerate((acc_p0[:], acc_p1[:, cols])):
+            if h == 0:
+                banks = [psum.tile([P, HALF], F32, name="acc_p0_%d" % b)[:] for b in range(N // P)]
+            else:
+                acc_p1 = psum.tile([P, N // P, HALF], F32, name="acc_p1")
+                banks = [acc_p1[:, b, :] for b in range(N // P)]
+            for b in range(N // P):
                 nc.tensor.matmul_mx(
-                    out=bank, lhsT=wb_w[:, b * P : (b + 1) * P].bitcast(E2M1),
+                    out=banks[b], lhsT=wb_w[:, b * P : (b + 1) * P].bitcast(E2M1),
                     lhsT_scale=wb_sc[:, b * P : (b + 1) * P],
                     rhs=codes[:].bitcast(E4M3), rhs_scale=code_sc[:], start=True, stop=True,
                 )
-            nc.scalar.copy(p_sb[0][:, cols], acc_p0[:])
-            if h == 1:
-                nc.scalar.copy(p_sb[1][:], acc_p1[:])
-            put(0, h * HALF, (h + 1) * HALF)
-        put(1, 0, O)
+            accs.extend(banks)
+
+        for b in range(N // P):
+            nc.scalar.copy(p_sb[:, b, 0:HALF], accs[b])
+        put_b(0, 0, HALF)
+        nc.scalar.copy(p_sb[:, :, HALF:O], acc_p1[:])
+        put_b(0, HALF, O)
+        put_b(1, 0, O)
+        for h in range(2):
+            for b in range(N // P):
+                put_a(b, h * HALF, (h + 1) * HALF)
 
         for b, lo, hi in ((0, 0, E), (1, 0, E // 2), (1, E // 2, E)):
             total = keep.tile([P, hi - lo], F32, name="total%d_%d" % (b, lo))

@@ -69,9 +69,9 @@ def tile_list_gatedgroupboard_chosen_one_pagetwice_kernel(
         loaded = keep.tile([P, 3, 2 * PACK], F32, name="loaded")
         nc.gpsimd.dma_start(loaded[:, 0, 0:PACK], sa.rearrange("(p t) one -> p (t one)", t=PACK))
 
-        boards = [keep.tile([P, C], F32, name="board%d" % t) for t in range(PACK)]
-        pages_a = [keep.tile([P, E], F32, name="page_a%d" % b) for b in range(N // P)]
-        pages_b = [keep.tile([P, E], F32, name="page_b%d" % b) for b in range(N // P)]
+        boards = [keep.tile([P, C], F32, name="board%d" % t, tag="board%d" % t) for t in range(PACK)]
+        pages_a = [keep.tile([P, E], F32, name="page_a0")]
+        pages_b = [keep.tile([P, E], F32, name="page_b0")]
         wb_sc = keep.tile([P, N], U8, name="wb_sc", align_bytes=64)
         nc.vector.memset(wb_sc[:].bitcast(I32), 0)
         for tile in boards + pages_a + pages_b:
@@ -152,6 +152,8 @@ def tile_list_gatedgroupboard_chosen_one_pagetwice_kernel(
                 ALU.mult,
             )
 
+        pages_a.append(keep.tile([P, E], F32, name="page_a1", tag="board1"))
+        pages_b.append(keep.tile([P, E], F32, name="page_b1", tag="board2"))
         p_sb = turns.tile([P, N // P, O], F32, name="p_sb", offset=0)
 
         def put_a(b, lo, hi):
@@ -168,6 +170,8 @@ def tile_list_gatedgroupboard_chosen_one_pagetwice_kernel(
             if h == 0:
                 hid = keep.tile([P, HALF * PACK], BF16, name="hid0", align_bytes=64)
                 product(hid, slice(0, HALF), PACK - 1)
+                for tile in (pages_a[1], pages_b[1]):
+                    nc.vector.memset(tile[:].bitcast(I32), 0)
                 nc.vector.tensor_tensor(
                     hid[:].rearrange("p (o t) -> p o t", t=PACK)[:, :, PACK - 1], last[:, 1, :], last[:, 0, :], ALU.mult
                 )

from contextlib import ExitStack

import concourse.mybir as mybir

K, T, J, R, V, C, O, N, E = 512, 1024, 256, 512, 1024, 512, 256, 256, 512
FLOPS = 2 * K * R * J + 2 * R * N * O

F32 = mybir.dt.float32
BF16 = mybir.dt.bfloat16
I32 = mybir.dt.int32
U32 = mybir.dt.uint32
U16 = mybir.dt.uint16
U8 = mybir.dt.uint8
E4M3 = mybir.dt.float8_e4m3fn_x4
E5M2 = mybir.dt.float8_e5m2_x4
E2M1 = mybir.dt.float4_e2m1fn_x4
ACT = mybir.ActivationFunctionType
ALU = mybir.AluOpType

P = 128
PACK = 4
QUAD = 32
HALF = O // 2
LIST_ROWS = 16


def tile_list_gatedgroupboard_chosen_one_pagetwice_kernel(
    tc, xt_words, xt_scales, wt_words, wt_scales, sa, sg, bg, wb_words, wb_scales,
    offs, offs2, offs3, offs4, offs5, offs6, offs7, out,
):
    nc = tc.nc
    with ExitStack() as ctx:
        keep = ctx.enter_context(tc.tile_pool(name="keep", bufs=1))
        turns = ctx.enter_context(tc.tile_pool(name="turns", bufs=1))
        psum = ctx.enter_context(tc.psum_pool(name="psum", bufs=1))

        def load_list(name, src):
            tile = keep.tile(list(src.shape), U16, name=name)
            nc.sync.dma_start(tile[:], src)
            return tile

        def load_scale_window(tile, src):
            rows = src[0].bitcast(I32)
            for q in range(P // QUAD):
                nc.sync.dma_start(
                    tile[QUAD * q : QUAD * (q + 1), :].bitcast(I32),
                    rows[PACK * q : PACK * (q + 1), :].partition_broadcast(QUAD // PACK),
                )

        warm_in = keep.tile([P, 1], F32, name="warm_in")
        warm_out = keep.tile([P, 1], F32, name="warm_out")
        nc.gpsimd.memset(warm_in[:], 0.0)
        nc.scalar.activation(out=warm_out[:], in_=warm_in[:], func=ACT.Sigmoid)

        wt_w = keep.tile([P, V], U16, name="wt_w")
        nc.sync.dma_start(wt_w[:].bitcast(I32), wt_words[0].bitcast(I32))
        list1 = load_list("list1", offs)
        wt_sc = keep.tile([P, V], U8, name="wt_sc")
        load_scale_window(wt_sc, wt_scales)
        list2 = load_list("list2", offs2)
        xt_w = turns.tile([P, T], I32, name="xt_w", offset=8192)
        nc.sync.dma_start(xt_w[:], xt_words[0].rearrange("p n t -> p (n t)").bitcast(I32))
        xt_sc = turns.tile([P, T], U8, name="xt_sc", offset=512)
        load_scale_window(xt_sc, xt_scales)
        list3 = load_list("list3", offs3)
        list4 = load_list("list4", offs4)
        list5 = load_list("list5", offs5)

        loaded = keep.tile([P, 3, 2 * PACK], F32, name="loaded")
        nc.gpsimd.dma_start(loaded[:, 0, 0:PACK], sa.rearrange("(p t) one -> p (t one)", t=PACK))

        boards = [keep.tile([P, C], F32, name="board%d" % t, tag="board%d" % t) for t in range(PACK)]
        pages_a = [keep.tile([P, E], F32, name="page_a0")]
        pages_b = [keep.tile([P, E], F32, name="page_b0")]
        wb_sc = keep.tile([P, N], U8, name="wb_sc", align_bytes=64)
        nc.vector.memset(wb_sc[:].bitcast(I32), 0)
        for tile in boards + pages_a + pages_b:
            nc.vector.memset(tile[:].bitcast(I32), 0)

        wb_w = keep.tile([P, N], U16, name="wb_w", align_bytes=64)
        nc.sync.dma_start(wb_w[:].bitcast(I32), wb_words[0].bitcast(I32))
        wb_rows = wb_scales[0].bitcast(I32)
        for q in range(P // QUAD):
            nc.sync.dma_start(
                wb_sc[QUAD * q : QUAD * q + PACK, :].bitcast(I32), wb_rows[PACK * q : PACK * (q + 1), :]
            )
        list6 = load_list("list6", offs6)
        list7 = load_list("list7", offs7)
        for i, src in ((1, sg), (2, bg)):
            nc.sync.dma_start(loaded[:, i, 0:PACK], src.rearrange("(p t) one -> p (t one)", t=PACK))
        consts = keep.tile([P, 3, PACK], F32, name="consts")
        nc.gpsimd.tensor_copy(consts[:], loaded[:, :, 0:PACK])

        wt_w_g = keep.tile([P, R], U16, name="wt_w_g")
        nc.vector.tensor_copy(wt_w_g[:], wt_w[:].indirect(list1[:]))
        wt_sc_g = keep.tile([P, R], U8, name="wt_sc_g")
        nc.vector.tensor_copy(wt_sc_g[:], wt_sc[:].indirect(list1[:]))
        xt_w_g = keep.tile([P, J], U32, name="xt_w_g", align_bytes=64)
        nc.vector.tensor_copy(xt_w_g[:], xt_w[:].bitcast(U32).indirect(list2[:]))
        xt_sc_g = keep.tile([P, J], U8, name="xt_sc_g", align_bytes=64)
        nc.vector.tensor_copy(xt_sc_g[:], xt_sc[:].indirect(list2[:]))

        wt_w_first = turns.tile([P, 1, P], U16, name="wt_w_first", offset=8192, align_bytes=64)
        wt_sc_first = turns.tile([P, 1, P], U8, name="wt_sc_first", offset=8192 + 256, align_bytes=64)
        wt_w_rest = turns.tile([P, PACK - 1, P], U16, name="wt_w_rest", offset=0, align_bytes=64)
        wt_sc_rest = turns.tile([P, PACK - 1, P], U8, name="wt_sc_rest", offset=768, align_bytes=64)
        w_by_t = wt_w_g[:].rearrange("p (m t) -> p t m", t=PACK)
        sc_by_t = wt_sc_g[:].rearrange("p (m t) -> p t m", t=PACK)
        nc.vector.tensor_copy(wt_w_first[:], w_by_t[:, 0:1, :])
        nc.vector.tensor_copy(wt_sc_first[:], sc_by_t[:, 0:1, :])
        nc.vector.tensor_copy(wt_w_rest[:], w_by_t[:, 1:PACK, :])
        nc.vector.tensor_copy(wt_sc_rest[:], sc_by_t[:, 1:PACK, :])

        looked = turns.tile([P, 2, PACK, O], F32, name="looked", offset=0)
        last = keep.tile([P, 2, HALF], F32, name="last", tag="last", align_bytes=64)

        def look(t, lo, hi, gate_out, picked_out):
            cols = slice(lo // LIST_ROWS, hi // LIST_ROWS)
            nc.scalar.activation(
                out=gate_out, in_=boards[t][:].indirect(list5[:, cols]), func=ACT.Sigmoid,
                bias=consts[:, 2, t : t + 1], scale=consts[:, 1, t : t + 1],
            )
            nc.scalar.activation(
                out=picked_out, in_=boards[t][:].indirect(list4[:, cols]), func=ACT.Copy,
                scale=consts[:, 0, t : t + 1],
            )

        a_sb = []
        for t in range(PACK):
            words = wt_w_first[:, 0, :] if t == 0 else wt_w_rest[:, t - 1, :]
            scales = wt_sc_first[:, 0, :] if t == 0 else wt_sc_rest[:, t - 1, :]
            acc = psum.tile([P, J], F32, name="acc_a%d" % t)
            nc.tensor.matmul_mx(
                out=acc[:], lhsT=words.bitcast(E2M1), lhsT_scale=scales,
                rhs=xt_w_g[:].bitcast(E5M2), rhs_scale=xt_sc_g[:], start=True, stop=True,
            )
            rows = keep.tile([P, J], F32, name="a_sb%d" % t)
            nc.scalar.copy(rows[:], acc[:])
            a_sb.append(rows)
        for t in range(PACK):
            nc.vector.tensor_copy(boards[t][:].indirect(list3[:]), a_sb[t][:])
            if t < PACK - 1:
                look(t, 0, O, looked[:, 0, t, :], looked[:, 1, t, :])
        look(PACK - 1, 0, HALF, last[:, 0, :], last[:, 1, :])
        look(PACK - 1, HALF, O, looked[:, 0, PACK - 1, HALF:O], looked[:, 1, PACK - 1, HALF:O])

        def product(hid, cols, slots):
            nc.vector.tensor_tensor(
                hid[:].rearrange("p (c i t) -> p c t i", i=4, t=PACK)[:, :, 0:slots, :],
                looked[:, 1, 0:slots, cols].rearrange("p t (c i) -> p c t i", i=4),
                looked[:, 0, 0:slots, cols].rearrange("p t (c i) -> p c t i", i=4),
                ALU.mult,
            )

        pages_a.append(keep.tile([P, E], F32, name="page_a1", tag="board1"))
        pages_b.append(keep.tile([P, E], F32, name="page_b1", tag="board2"))
        p_sb = turns.tile([P, N // P, O], F32, name="p_sb", offset=0)

        def put_a(b, lo, hi):
            nc.vector.tensor_copy(pages_a[b][:].indirect(list6[:, lo // LIST_ROWS : hi // LIST_ROWS]), p_sb[:, b, lo:hi])

        def put_b(b, lo, hi):
            nc.scalar.activation(
                out=pages_b[b][:].indirect(list7[:, lo // LIST_ROWS : hi // LIST_ROWS]), in_=p_sb[:, b, lo:hi],
                func=ACT.Copy,
            )

        accs = []
        for h in range(2):
            if h == 0:
                hid = keep.tile([P, HALF * PACK], BF16, name="hid0", align_bytes=64)
                product(hid, slice(0, HALF), PACK - 1)
                for tile in (pages_a[1], pages_b[1]):
                    nc.vector.memset(tile[:].bitcast(I32), 0)
                nc.vector.tensor_tensor(
                    hid[:].rearrange("p (o t) -> p o t", t=PACK)[:, :, PACK - 1], last[:, 1, :], last[:, 0, :], ALU.mult
                )
            else:
                hid = keep.tile([P, HALF * PACK], BF16, name="hid1", tag="last", align_bytes=64)
                product(hid, slice(HALF, O), PACK)
            codes = keep.tile([P, HALF], U32, name="codes%d" % h, align_bytes=64)
            code_sc = keep.tile([P, HALF], U8, name="code_sc%d" % h, align_bytes=64)
            nc.vector.quantize_mx(out=codes[:].bitcast(E4M3), scales=code_sc[:], in_=hid[:])
            if h == 0:
                banks = [psum.tile([P, HALF], F32, name="acc_p0_%d" % b)[:] for b in range(N // P)]
            else:
                acc_p1 = psum.tile([P, N // P, HALF], F32, name="acc_p1")
                banks = [acc_p1[:, b, :] for b in range(N // P)]
            for b in range(N // P):
                nc.tensor.matmul_mx(
                    out=banks[b], lhsT=wb_w[:, b * P : (b + 1) * P].bitcast(E2M1),
                    lhsT_scale=wb_sc[:, b * P : (b + 1) * P],
                    rhs=codes[:].bitcast(E4M3), rhs_scale=code_sc[:], start=True, stop=True,
                )
            accs.extend(banks)

        for b in range(N // P):
            nc.scalar.copy(p_sb[:, b, 0:HALF], accs[b])
        put_b(0, 0, HALF)
        nc.scalar.copy(p_sb[:, :, HALF:O], acc_p1[:])
        put_b(0, HALF, O)
        put_b(1, 0, O)
        for h in range(2):
            for b in range(N // P):
                put_a(b, h * HALF, (h + 1) * HALF)

        for b, lo, hi in ((0, 0, E), (1, 0, E // 2), (1, E // 2, E)):
            total = keep.tile([P, hi - lo], F32, name="total%d_%d" % (b, lo))
            nc.vector.tensor_tensor(total[:], pages_a[b][:, lo:hi], pages_b[b][:, lo:hi], ALU.add)
            nc.sync.dma_start(out[b * P : (b + 1) * P, lo:hi], total[:])
